import numpy as np
import ml_dtypes


def mxq(x, axis, fmt="e4m3"):
    dtype, down = {"e4m3": (ml_dtypes.float8_e4m3fn, 7), "e5m2": (ml_dtypes.float8_e5m2, 14)}[fmt]
    v = np.moveaxis(np.asarray(x, np.float32).astype(ml_dtypes.bfloat16).astype(np.float64), axis, -1)
    blocks = v.reshape(v.shape[:-1] + (-1, 32))
    amax = np.abs(blocks).max(-1, keepdims=True)
    byte = np.maximum(np.where(amax > 0, np.frexp(amax)[1] - 1 + 127, 0) - down, 1)
    scale = np.exp2(byte - 127.0)
    codes = (blocks / scale).astype(np.float32).astype(dtype).astype(np.float64)
    return np.moveaxis((codes * scale).reshape(v.shape), -1, axis)


WIDE = False


def mx_kscale(k):
    if not WIDE:
        return np.ones(k)
    levels = np.array([10, -10, 5, -5, 0])
    if k % 512:
        return np.exp2(np.random.permutation(np.resize(levels, k // 32))).repeat(32)
    a = np.empty((k // 512, 16))
    for p in range(k // 512):
        a[p, :8] = np.random.permutation(np.resize(levels, 8))
        for g in range(8):
            far = levels[np.abs(levels - a[p, g]) >= 10]
            a[p, g + 8] = far[np.random.randint(len(far))]
    return np.exp2(a.ravel()).repeat(32)


def f64(x):
    return np.asarray(x).astype(np.float64)


def striped(idx):
    return np.tile(idx.reshape(-1, 16).T, (8, 1)).astype(np.uint16)


def unstriped(offs):
    return offs[:16].T.reshape(-1).astype(np.int64)


E2M1 = np.array([0.0, 0.5, 1.0, 1.5, 2.0, 3.0, 4.0, 6.0, -0.0, -0.5, -1.0, -1.5, -2.0, -3.0, -4.0, -6.0])


def pack_weight(w, fmt):
    k, n = w.shape
    w = f64(np.asarray(w, np.float32).astype(ml_dtypes.bfloat16)).reshape(k // 32, 32, n)
    amax = np.abs(w).max(1)
    if fmt == "e4m3":
        byte = np.frexp(amax)[1] - 1 + 127 - 7
    else:
        mant, ex = np.frexp(amax / 6.0)
        byte = np.where(mant > 0.5, ex, ex - 1) + 127
    byte = np.clip(np.where(amax > 0, byte, 1), 1, 254)
    scaled = (w * np.exp2(127.0 - byte)[:, None, :]).reshape(k, n).astype(np.float32)
    by_word = np.ascontiguousarray(scaled.reshape(k // 512, 128, 4, n).transpose(0, 1, 3, 2))
    if fmt == "e4m3":
        words = by_word.astype(ml_dtypes.float8_e4m3fn).view(np.uint8)
    else:
        c = by_word.astype(ml_dtypes.float4_e2m1fn).view(np.uint8) & 0xF
        words = (c[..., 0::2] | (c[..., 1::2] << 4)).reshape(k // 512, 128, 2 * n)
    return np.ascontiguousarray(words), np.ascontiguousarray(byte.astype(np.uint8).reshape(k // 512, 16, n))


def unpack_weight(words, scales, fmt):
    g, _, n = scales.shape
    words = np.ascontiguousarray(words).reshape(g, 128, n, -1)
    if fmt == "e4m3":
        vals = words.view(ml_dtypes.float8_e4m3fn).astype(np.float64)
    else:
        nib = np.empty((g, 128, n, 4), np.uint8)
        nib[..., 0::2] = words & 0xF
        nib[..., 1::2] = words >> 4
        vals = E2M1[nib]
    vals = vals * np.repeat(np.exp2(scales.astype(np.float64) - 127.0), 8, axis=1)[..., None]
    return vals.transpose(0, 1, 3, 2).reshape(g * 512, n)


def gelu(v):
    return 0.5 * v * (1.0 + np.tanh(np.sqrt(2.0 / np.pi) * (v + 0.044715 * v**3)))


K, T, S, H, T3, S2, T2 = 1024, 2048, 512, 1024, 1024, 512, 1024

def setup_inputs():
    n = np.random.standard_normal
    s = mx_kscale(K)[:, None]
    u = mx_kscale(H)[:, None]
    tab_words, tab_scales = pack_weight(n((K, T)) * s, "e4m3")
    tab2_words, tab2_scales = pack_weight(n((H, T3)) / np.sqrt(H) / u, "e4m3")
    wter = (n((K, H)) / np.sqrt(K) / s * u.T).astype(np.float32)
    wnav_words, wnav_scales = pack_weight(n((K, H)) / np.sqrt(K) / s * u.T, "e2m1")
    wleg_words, wleg_scales = pack_weight(n((K, H)) / np.sqrt(K) / s * u.T, "e4m3")
    return {
        "tab_words": tab_words, "tab_scales": tab_scales,
        "offs": striped(np.random.permutation(T)[:S]),
        "tab2_words": tab2_words, "tab2_scales": tab2_scales,
        "offs2": striped(np.random.permutation(T3)[:S2]),
        "offs3": striped(np.random.permutation(T2)[:S]),
        "wter": wter,
        "wnav_words": wnav_words, "wnav_scales": wnav_scales,
        "wleg_words": wleg_words, "wleg_scales": wleg_scales,
        "gain": n(H).astype(np.float32),
        "limit": (0.3 + n((S2, S))).astype(np.float32),
        "arch": (0.8 * n(S2)).astype(np.float32),
        "wgo": np.exp(0.3 * n((128, S))).astype(np.float32),
        "page1": n((S2, T2)).astype(np.float32),
    }

def reference(tab_words, tab_scales, offs, tab2_words, tab2_scales, offs2, offs3, wter, wnav_words, wnav_scales, wleg_words, wleg_scales, gain, limit, arch, wgo, page1):
    v = unpack_weight(tab_words, tab_scales, "e4m3")[:, unstriped(offs)]
    v2 = unpack_weight(tab2_words, tab2_scales, "e4m3")[:, unstriped(offs2)]
    wt = mxq(f64(wter), 0, "e4m3")
    wn = unpack_weight(wnav_words, wnav_scales, "e2m1")
    wl = unpack_weight(wleg_words, wleg_scales, "e4m3")
    ter = wt.T @ v
    nav = wn.T @ v
    leg = wl.T @ v
    h = np.maximum(ter, nav) * f64(gain)[:, None] + leg
    hq = mxq(h, 0, "e4m3")
    e = v2.T @ hq
    y = np.minimum(e, f64(limit)) + f64(arch)[:, None]
    out = f64(page1).copy()
    out[:, unstriped(offs3)] = np.tile(f64(wgo), (S2 // 128, 1)) * y
    return out

@@ -1,0 +1,343 @@
+from contextlib import ExitStack
+
+import concourse.mybir as mybir
+
+K, T, S, H, T3, S2, T2 = 1024, 2048, 512, 1024, 1024, 512, 1024
+FLOPS = 2 * (3 * K * H * S + H * S2 * S)
+
+F32 = mybir.dt.float32
+BF16 = mybir.dt.bfloat16
+I32 = mybir.dt.int32
+U32 = mybir.dt.uint32
+U16 = mybir.dt.uint16
+U8 = mybir.dt.uint8
+FP8X4 = mybir.dt.float8_e4m3fn_x4
+FP4X4 = mybir.dt.float4_e2m1fn_x4
+ALU = mybir.AluOpType
+ACT = mybir.ActivationFunctionType
+
+P = 128
+PACK = 4
+PASS = P * PACK
+KP = K // PASS
+HP = H // PASS
+HALF = S // 2
+MT = S2 // P
+LEG_ROW = 4
+TAB2_ROW = 8
+VECTOR_SHARE = {(0, 0): 0, (1, 0): 64, (0, 1): 0, (1, 1): 64}
+
+
+def tile_list_orienteering_leg_scores_kernel(
+    tc, tab_words, tab_scales, offs, tab2_words, tab2_scales, offs2, offs3, wter,
+    wnav_words, wnav_scales, wleg_words, wleg_scales, gain, limit, arch, wgo, page1, out,
+):
+    nc = tc.nc
+    with ExitStack() as ctx:
+        keep = ctx.enter_context(tc.tile_pool(name="keep", bufs=1))
+        ring = ctx.enter_context(tc.tile_pool(name="ring", bufs=2))
+        psum = ctx.enter_context(tc.psum_pool(name="psum", bufs=1))
+
+        def held(shape, dtype, name):
+            return keep.tile(shape, dtype, name=name, align_bytes=64)
+
+        list1 = keep.tile([P, S // 16], U16, name="list1")
+        list2 = keep.tile([P, S2 // 16], U16, name="list2")
+        list3 = keep.tile([P, S // 16], U16, name="list3")
+
+        tab_w = [held([P, T], I32, f"tab_w{a}") for a in range(KP)]
+        tab_s = held([P, KP, T], U8, "tab_s")
+        tab2_w = [held([P, T3], I32, f"tab2_w{b}") for b in range(HP)]
+        tab2_s = held([P, T3], U8, "tab2_s")
+        w_s = held([P, KP, H], U8, "w_s")
+        nav_w = [held([P, KP, 2 * PASS], U8, f"nav_w{b}") for b in range(HP)]
+        leg_w = [held([P, KP, PASS], I32, f"leg_w{b}") for b in range(HP)]
+        ter_f = {(a, b): held([P, PACK, PASS], F32, f"ter_f{a}{b}") for a in range(KP) for b in range(HP)}
+        gain_t = held([P, HP, PACK], F32, "gain_t")
+        arch_t = held([P, MT], F32, "arch_t")
+        wgo_t = held([P, S], F32, "wgo_t")
+        lim = [held([P, S], F32, f"lim{t}") for t in range(MT)]
+        page = [held([P, T2], F32, f"page{t}") for t in range(MT)]
+
+        nc.gpsimd.memset(tab_s[:, 0, :].bitcast(I32), 0)
+        nc.vector.memset(tab_s[:, 1, :].bitcast(I32), 0)
+        nc.vector.memset(w_s[:].bitcast(I32), 0)
+        nc.vector.memset(tab2_s[:].bitcast(I32), 0)
+
+        def load_scale_rows(dst, row, src, q):
+            nc.sync.dma_start(
+                dst[32 * q + row : 32 * q + row + 4].bitcast(I32),
+                src[:, 4 * q : 4 * q + 4, :].rearrange("a r t -> r a t").bitcast(I32),
+            )
+
+        def load_tab2_scales(q):
+            nc.sync.dma_start(
+                tab2_s[32 * q + TAB2_ROW : 32 * q + TAB2_ROW + 8].bitcast(I32),
+                tab2_scales[:, 4 * q : 4 * q + 4, :].bitcast(I32),
+            )
+
+        def load_tab(a, c0, c1):
+            nc.sync.dma_start(tab_w[a][:, c0:c1], tab_words[a, :, c0:c1, :].rearrange("p t i -> p (t i)").bitcast(I32))
+
+
+        def load_nav(b):
+            nc.sync.dma_start(
+                nav_w[b][:].bitcast(I32),
+                wnav_words[:, :, 2 * PASS * b : 2 * PASS * (b + 1)].rearrange("a p n -> p a n").bitcast(I32),
+            )
+
+        def load_leg(b):
+            nc.sync.dma_start(
+                leg_w[b][:],
+                wleg_words[:, :, PASS * b : PASS * (b + 1), :].rearrange("a p c i -> p a (c i)").bitcast(I32),
+            )
+
+        def load_ter(a, b):
+            nc.sync.dma_start(
+                ter_f[a, b][:],
+                wter[PASS * a : PASS * (a + 1), PASS * b : PASS * (b + 1)].rearrange("(p j) c -> p j c", j=PACK),
+            )
+
+        nc.sync.dma_start(list1[:], offs)
+        nc.sync.dma_start(list2[:], offs2)
+        nc.sync.dma_start(list3[:], offs3)
+        for c in range(0, T, T // 4):
+            load_tab(0, c, c + T // 4)
+        load_nav(0)
+        for q in range(4):
+            load_scale_rows(tab_s, 0, tab_scales, q)
+        load_ter(0, 0)
+        for q in range(4):
+            load_scale_rows(w_s, 0, wnav_scales, q)
+        load_ter(1, 0)
+        for q in range(4):
+            load_scale_rows(w_s, LEG_ROW, wleg_scales, q)
+        load_tab(1, 0, T)
+        nc.sync.dma_start(gain_t[:], gain.rearrange("(b p i) -> p b i", b=HP, i=PACK))
+        load_leg(0)
+        load_nav(1)
+        load_leg(1)
+        for q in range(4):
+            load_tab2_scales(q)
+        load_ter(0, 1)
+        load_ter(1, 1)
+        for b in range(HP):
+            nc.sync.dma_start(tab2_w[b][:], tab2_words[b].rearrange("p t i -> p (t i)").bitcast(I32))
+        with nc.allow_non_contiguous_dma(reason="one value of arch to a partition and row tile"):
+            nc.sync.dma_start(arch_t[:], arch.rearrange("(t p) -> p t", p=P))
+        nc.sync.dma_start(wgo_t[:], wgo)
+        for t in range(MT):
+            nc.sync.dma_start(lim[t][:], limit[P * t : P * (t + 1), :])
+            nc.sync.dma_start(page[t][:], page1[P * t : P * (t + 1), :])
+
+        v_w = [held([P, S], U32, f"v_w{a}") for a in range(KP)]
+        v_s = [held([P, S], U8, f"v_s{a}") for a in range(KP)]
+
+        def gather_words(a, c0, c1):
+            nc.vector.tensor_copy(v_w[a][:, c0:c1], tab_w[a][:].bitcast(U32).indirect(list1[:, c0 // 16 : c1 // 16]))
+
+        def gather_scales(a):
+            nc.vector.tensor_copy(v_s[a][:], tab_s[:, a, :].indirect(list1[:]))
+
+        v2_w = [held([P, S2], U32, f"v2_w{b}") for b in range(HP)]
+        v2_s = held([P, S2], U8, "v2_s")
+
+        nav_d = [held([P, KP, 2 * PASS], U8, f"nav_d{b}") for b in range(HP)]
+        leg_d = [held([P, KP, PASS], U32, f"leg_d{b}") for b in range(HP)]
+        w_sd = [held([P, KP, PASS], U8, f"w_sd{b}") for b in range(HP)]
+        ter_q = {ab: held([P, PASS], U32, f"ter_q{ab[0]}{ab[1]}") for ab in ter_f}
+        ter_s = {ab: held([P, PASS], U8, f"ter_s{ab[0]}{ab[1]}") for ab in ter_f}
+        nav_f = {(b, u): held([P, PACK, HALF], F32, f"nav_f{b}{u}") for b in range(HP) for u in range(2)}
+        h_q = {(b, u): held([P, HALF], U32, f"h_q{b}{u}") for b in range(HP) for u in range(2)}
+        h_s = {(b, u): held([P, HALF], U8, f"h_s{b}{u}") for b in range(HP) for u in range(2)}
+
+        def deal_scales(b):
+            nc.vector.tensor_copy(
+                w_sd[b][:].rearrange("p a (i m) -> p a i m", i=PACK),
+                w_s[:, :, PASS * b : PASS * (b + 1)].rearrange("p a (m i) -> p a i m", i=PACK),
+            )
+
+        def deal_nav(b):
+            nc.scalar.copy(
+                nav_d[b][:].bitcast(U16).rearrange("p a (i m) -> p a i m", i=PACK),
+                nav_w[b][:].bitcast(U16).rearrange("p a (m i) -> p a i m", i=PACK),
+            )
+
+        def deal_leg(b):
+            nc.scalar.copy(
+                leg_d[b][:].rearrange("p a (i m) -> p a m i", i=PACK),
+                leg_w[b][:].bitcast(U32).rearrange("p a (m i) -> p a m i", i=PACK),
+            )
+
+        def round_ter(a, b):
+            grouped = ring.tile([P, PACK * PASS], BF16, name="grouped", align_bytes=64, bufs=4)
+            dst = grouped[:].rearrange("p (i m j) -> p m j i", i=PACK, j=PACK)
+            src = ter_f[a, b][:].rearrange("p j (m i) -> p m j i", i=PACK)
+            cut = VECTOR_SHARE[a, b]
+            if cut > 0:
+                nc.vector.tensor_copy(dst[:, :cut], src[:, :cut])
+            if cut < P:
+                nc.scalar.copy(dst[:, cut:], src[:, cut:])
+            return grouped
+
+        def quantise_ter(a, b, grouped):
+            nc.vector.quantize_mx(out=ter_q[a, b][:].bitcast(FP8X4), scales=ter_s[a, b][:], in_=grouped[:])
+
+        def pair_product(name, bufs, words, scales, i0, u):
+            bank = psum.tile([P, 2, HALF], F32, name=name, bufs=bufs)
+            cols = slice(HALF * u, HALF * (u + 1))
+            for a in range(KP):
+                for d in range(2):
+                    i = i0 + d
+                    nc.tensor.matmul_mx(
+                        out=bank[:, d, :],
+                        lhsT=words(a, i),
+                        lhsT_scale=scales(a, i),
+                        rhs=v_w[a][:, cols].bitcast(FP8X4),
+                        rhs_scale=v_s[a][:, cols],
+                        start=(a == 0 and d == 0),
+                        stop=(a == KP - 1 and d == 1),
+                    )
+            return bank
+
+        def nav_stage(b, u):
+            for i0 in (0, 2):
+                bank = pair_product(
+                    "bank_a", 2,
+                    lambda a, i: nav_d[b][:, a, 2 * P * i : 2 * P * (i + 1)].bitcast(FP4X4),
+                    lambda a, i: w_sd[b][:, a, P * i : P * (i + 1)],
+                    i0, u,
+                )
+                nc.scalar.copy(nav_f[b, u][:, i0 : i0 + 2, :], bank[:])
+
+        def join_max(b, u):
+            top = ring.tile([P, PACK, HALF], F32, name="top", bufs=4)
+            for i0 in (0, 2):
+                bank = pair_product(
+                    "bank_t", 3,
+                    lambda a, i: ter_q[a, b][:, P * i : P * (i + 1)].bitcast(FP8X4),
+                    lambda a, i: ter_s[a, b][:, P * i : P * (i + 1)],
+                    i0, u,
+                )
+                nc.vector.tensor_tensor(top[:, i0 : i0 + 2, :], bank[:], nav_f[b, u][:, i0 : i0 + 2, :], ALU.max)
+            return top
+
+        def join_leg(b, u, top):
+            planes = ring.tile([P, PACK, HALF], BF16, name="planes", bufs=4)
+            for i0 in (0, 2):
+                bank = pair_product(
+                    "bank_l", 3,
+                    lambda a, i: leg_d[b][:, a, P * i : P * (i + 1)].bitcast(FP8X4),
+                    lambda a, i: w_sd[b][LEG_ROW:, a, P * i : P * (i + 1)],
+                    i0, u,
+                )
+                for d in range(2):
+                    i = i0 + d
+                    nc.vector.scalar_tensor_tensor(
+                        planes[:, i, :], top[:, i, :], gain_t[:, b, i : i + 1], bank[:, d, :], ALU.mult, ALU.add
+                    )
+            return planes
+
+        def weave(planes):
+            woven = ring.tile([P, PACK * HALF], BF16, name="woven", align_bytes=64, bufs=4)
+            nc.scalar.copy(
+                woven[:].rearrange("p (c n i) -> p c i n", n=4, i=PACK),
+                planes[:].rearrange("p i (c n) -> p c i n", n=4),
+            )
+            return woven
+
+        def quantise_h(b, u, woven):
+            nc.vector.quantize_mx(out=h_q[b, u][:].bitcast(FP8X4), scales=h_s[b, u][:], in_=woven[:])
+
+        cap = [held([P, S], F32, f"cap{t}") for t in range(MT)]
+
+        def score(u):
+            cols = slice(HALF * u, HALF * (u + 1))
+            capped = []
+            for t0 in (0, 2):
+                bank = psum.tile([P, 2, HALF], F32, name="bank_a", bufs=2)
+                for b in range(HP):
+                    for d in range(2):
+                        t = t0 + d
+                        nc.tensor.matmul_mx(
+                            out=bank[:, d, :],
+                            lhsT=v2_w[b][:, P * t : P * (t + 1)].bitcast(FP8X4),
+                            lhsT_scale=v2_s[TAB2_ROW + 4 * b :, P * t : P * (t + 1)],
+                            rhs=h_q[b, u][:].bitcast(FP8X4),
+                            rhs_scale=h_s[b, u][:],
+                            start=(b == 0 and d == 0),
+                            stop=(b == HP - 1 and d == 1),
+                        )
+                for d in range(2):
+                    t = t0 + d
+                    y = ring.tile([P, HALF], F32, name="y", bufs=8)
+                    nc.vector.scalar_tensor_tensor(
+                        y[:], bank[:, d, :], arch_t[:, t : t + 1], cap[t][:, cols], ALU.add, ALU.min
+                    )
+                    capped.append(y)
+            return capped
+
+        def place(u, capped):
+            cols = slice(HALF * u, HALF * (u + 1))
+            entries = list3[:, HALF // 16 * u : HALF // 16 * (u + 1)]
+            for t in range(MT):
+                nc.vector.tensor_tensor(page[t][:].indirect(entries), capped[t][:], wgo_t[:, cols], ALU.mult)
+                if u == 1:
+                    nc.sync.dma_start(out[P * t : P * (t + 1), :], page[t][:])
+
+        def add_arch(t):
+            nc.scalar.activation(cap[t][:], lim[t][:], ACT.Identity, bias=arch_t[:, t : t + 1])
+
+        def gather_tab2(b):
+            nc.vector.tensor_copy(v2_w[b][:], tab2_w[b][:].bitcast(U32).indirect(list2[:]))
+
+        gather_words(0, 0, S)
+        deal_nav(0)
+        g00 = round_ter(0, 0)
+        gather_scales(0)
+        gather_scales(1)
+        g10 = round_ter(1, 0)
+        quantise_ter(0, 0, g00)
+        deal_scales(0)
+        quantise_ter(1, 0, g10)
+        gather_words(1, 0, HALF)
+        gather_words(1, HALF, S)
+        nav_stage(0, 0)
+        top00 = join_max(0, 0)
+        nav_stage(0, 1)
+        deal_leg(0)
+        top01 = join_max(0, 1)
+        deal_scales(1)
+        deal_nav(1)
+        p00 = join_leg(0, 0, top00)
+        p01 = join_leg(0, 1, top01)
+        nav_stage(1, 0)
+        g01 = round_ter(0, 1)
+        nav_stage(1, 1)
+        g11 = round_ter(1, 1)
+        deal_leg(1)
+        quantise_ter(0, 1, g01)
+        quantise_ter(1, 1, g11)
+        top10 = join_max(1, 0)
+        p10 = join_leg(1, 0, top10)
+        w00 = weave(p00)
+        w10 = weave(p10)
+        nc.vector.tensor_copy(v2_s[:], tab2_s[:].indirect(list2[:]))
+        gather_tab2(0)
+        gather_tab2(1)
+        top11 = join_max(1, 1)
+        p11 = join_leg(1, 1, top11)
+        add_arch(0)
+        add_arch(1)
+        w01 = weave(p01)
+        w11 = weave(p11)
+        add_arch(2)
+        add_arch(3)
+        quantise_h(0, 0, w00)
+        quantise_h(1, 0, w10)
+        first = score(0)
+        quantise_h(0, 1, w01)
+        quantise_h(1, 1, w11)
+        second = score(1)
+        place(0, first)
+        place(1, second)

@@ -21,11 +21,10 @@ PACK = 4
 PASS = P * PACK
 KP = K // PASS
 HP = H // PASS
-HALF = S // 2
 MT = S2 // P
+QUADS = 4
 LEG_ROW = 4
 TAB2_ROW = 8
-VECTOR_SHARE = {(0, 0): 0, (1, 0): 64, (0, 1): 0, (1, 1): 64}
 
 
 def tile_list_orienteering_leg_scores_kernel(
@@ -35,8 +34,7 @@ def tile_list_orienteering_leg_scores_kernel(
     nc = tc.nc
     with ExitStack() as ctx:
         keep = ctx.enter_context(tc.tile_pool(name="keep", bufs=1))
-        ring = ctx.enter_context(tc.tile_pool(name="ring", bufs=2))
-        psum = ctx.enter_context(tc.psum_pool(name="psum", bufs=1))
+        psum = ctx.enter_context(tc.psum_pool(name="psum", bufs=8))
 
         def held(shape, dtype, name):
             return keep.tile(shape, dtype, name=name, align_bytes=64)
@@ -49,10 +47,10 @@ def tile_list_orienteering_leg_scores_kernel(
         tab_s = held([P, KP, T], U8, "tab_s")
         tab2_w = [held([P, T3], I32, f"tab2_w{b}") for b in range(HP)]
         tab2_s = held([P, T3], U8, "tab2_s")
-        w_s = held([P, KP, H], U8, "w_s")
+        nav_s = held([P, KP, H], U8, "nav_s")
+        leg_s = held([P, H], U8, "leg_s")
         nav_w = [held([P, KP, 2 * PASS], U8, f"nav_w{b}") for b in range(HP)]
         leg_w = [held([P, KP, PASS], I32, f"leg_w{b}") for b in range(HP)]
-        ter_f = {(a, b): held([P, PACK, PASS], F32, f"ter_f{a}{b}") for a in range(KP) for b in range(HP)}
         gain_t = held([P, HP, PACK], F32, "gain_t")
         arch_t = held([P, MT], F32, "arch_t")
         wgo_t = held([P, S], F32, "wgo_t")
@@ -61,24 +59,26 @@ def tile_list_orienteering_leg_scores_kernel(
 
         nc.gpsimd.memset(tab_s[:, 0, :].bitcast(I32), 0)
         nc.vector.memset(tab_s[:, 1, :].bitcast(I32), 0)
-        nc.vector.memset(w_s[:].bitcast(I32), 0)
+        nc.vector.memset(nav_s[:].bitcast(I32), 0)
+        nc.vector.memset(leg_s[:].bitcast(I32), 0)
         nc.vector.memset(tab2_s[:].bitcast(I32), 0)
 
-        def load_scale_rows(dst, row, src, q):
-            nc.sync.dma_start(
-                dst[32 * q + row : 32 * q + row + 4].bitcast(I32),
-                src[:, 4 * q : 4 * q + 4, :].rearrange("a r t -> r a t").bitcast(I32),
-            )
+        def load_scales_side_by_side(dst, src):
+            for r in range(4):
+                nc.sync.dma_start(
+                    dst[r:P:32].bitcast(I32),
+                    src[:, r:16:4, :].rearrange("a q t -> q a t").bitcast(I32),
+                )
 
-        def load_tab2_scales(q):
-            nc.sync.dma_start(
-                tab2_s[32 * q + TAB2_ROW : 32 * q + TAB2_ROW + 8].bitcast(I32),
-                tab2_scales[:, 4 * q : 4 * q + 4, :].bitcast(I32),
-            )
+        def load_scales_stacked(dst, row, src):
+            for q in range(QUADS):
+                nc.sync.dma_start(
+                    dst[32 * q + row : 32 * q + row + 8].bitcast(I32),
+                    src[:, 4 * q : 4 * q + 4, :].bitcast(I32),
+                )
 
         def load_tab(a, c0, c1):
             nc.sync.dma_start(tab_w[a][:, c0:c1], tab_words[a, :, c0:c1, :].rearrange("p t i -> p (t i)").bitcast(I32))
-
 
         def load_nav(b):
             nc.sync.dma_start(
@@ -92,11 +92,11 @@ def tile_list_orienteering_leg_scores_kernel(
                 wleg_words[:, :, PASS * b : PASS * (b + 1), :].rearrange("a p c i -> p a (c i)").bitcast(I32),
             )
 
-        def load_ter(a, b):
-            nc.sync.dma_start(
-                ter_f[a, b][:],
-                wter[PASS * a : PASS * (a + 1), PASS * b : PASS * (b + 1)].rearrange("(p j) c -> p j c", j=PACK),
-            )
+        def load_ter(a, b, m0, m1):
+            raw = held([P, PACK, PACK * (m1 - m0)], F32, f"ter_raw{a}{b}_{m0}")
+            cols = slice(PASS * b + PACK * m0, PASS * b + PACK * m1)
+            nc.sync.dma_start(raw[:], wter[PASS * a : PASS * (a + 1), cols].rearrange("(p j) c -> p j c", j=PACK))
+            return raw
 
         nc.sync.dma_start(list1[:], offs)
         nc.sync.dma_start(list2[:], offs2)
@@ -104,57 +104,66 @@ def tile_list_orienteering_leg_scores_kernel(
         for c in range(0, T, T // 4):
             load_tab(0, c, c + T // 4)
         load_nav(0)
-        for q in range(4):
-            load_scale_rows(tab_s, 0, tab_scales, q)
-        load_ter(0, 0)
-        for q in range(4):
-            load_scale_rows(w_s, 0, wnav_scales, q)
-        load_ter(1, 0)
-        for q in range(4):
-            load_scale_rows(w_s, LEG_ROW, wleg_scales, q)
+        load_scales_side_by_side(tab_s, tab_scales)
+        raw00 = load_ter(0, 0, 0, P)
+        load_scales_side_by_side(nav_s, wnav_scales)
         load_tab(1, 0, T)
-        nc.sync.dma_start(gain_t[:], gain.rearrange("(b p i) -> p b i", b=HP, i=PACK))
+        raw10a = load_ter(1, 0, 0, P // 2)
+        raw10b = load_ter(1, 0, P // 2, P)
         load_leg(0)
+        load_scales_stacked(leg_s, LEG_ROW, wleg_scales)
         load_nav(1)
+        nc.sync.dma_start(gain_t[:], gain.rearrange("(b p i) -> p b i", b=HP, i=PACK))
+        raw01 = load_ter(0, 1, 0, P)
+        raw11 = load_ter(1, 1, 0, P)
         load_leg(1)
-        for q in range(4):
-            load_tab2_scales(q)
-        load_ter(0, 1)
-        load_ter(1, 1)
-        for b in range(HP):
-            nc.sync.dma_start(tab2_w[b][:], tab2_words[b].rearrange("p t i -> p (t i)").bitcast(I32))
+        load_scales_stacked(tab2_s, TAB2_ROW, tab2_scales)
         with nc.allow_non_contiguous_dma(reason="one value of arch to a partition and row tile"):
             nc.sync.dma_start(arch_t[:], arch.rearrange("(t p) -> p t", p=P))
         nc.sync.dma_start(wgo_t[:], wgo)
         for t in range(MT):
             nc.sync.dma_start(lim[t][:], limit[P * t : P * (t + 1), :])
+        for b in range(HP):
+            nc.sync.dma_start(tab2_w[b][:], tab2_words[b].rearrange("p t i -> p (t i)").bitcast(I32))
+        for t in range(MT):
             nc.sync.dma_start(page[t][:], page1[P * t : P * (t + 1), :])
 
         v_w = [held([P, S], U32, f"v_w{a}") for a in range(KP)]
         v_s = [held([P, S], U8, f"v_s{a}") for a in range(KP)]
-
-        def gather_words(a, c0, c1):
-            nc.vector.tensor_copy(v_w[a][:, c0:c1], tab_w[a][:].bitcast(U32).indirect(list1[:, c0 // 16 : c1 // 16]))
-
-        def gather_scales(a):
-            nc.vector.tensor_copy(v_s[a][:], tab_s[:, a, :].indirect(list1[:]))
-
         v2_w = [held([P, S2], U32, f"v2_w{b}") for b in range(HP)]
         v2_s = held([P, S2], U8, "v2_s")
-
         nav_d = [held([P, KP, 2 * PASS], U8, f"nav_d{b}") for b in range(HP)]
         leg_d = [held([P, KP, PASS], U32, f"leg_d{b}") for b in range(HP)]
-        w_sd = [held([P, KP, PASS], U8, f"w_sd{b}") for b in range(HP)]
-        ter_q = {ab: held([P, PASS], U32, f"ter_q{ab[0]}{ab[1]}") for ab in ter_f}
-        ter_s = {ab: held([P, PASS], U8, f"ter_s{ab[0]}{ab[1]}") for ab in ter_f}
-        nav_f = {(b, u): held([P, PACK, HALF], F32, f"nav_f{b}{u}") for b in range(HP) for u in range(2)}
-        h_q = {(b, u): held([P, HALF], U32, f"h_q{b}{u}") for b in range(HP) for u in range(2)}
-        h_s = {(b, u): held([P, HALF], U8, f"h_s{b}{u}") for b in range(HP) for u in range(2)}
+        nav_sd = [held([P, KP, PASS], U8, f"nav_sd{b}") for b in range(HP)]
+        leg_sd = held([P, HP, PASS], U8, "leg_sd")
+        ter_q = {(a, b): held([P, PASS], U32, f"ter_q{a}{b}") for a in range(KP) for b in range(HP)}
+        ter_s = {(a, b): held([P, PASS], U8, f"ter_s{a}{b}") for a in range(KP) for b in range(HP)}
+        top = [held([P, S], F32, f"top{i}") for i in range(PACK)]
+        planes = [held([P, PACK, S], BF16, f"planes{b}") for b in range(HP)]
+        h_q = [held([P, S], U32, f"h_q{b}") for b in range(HP)]
+        h_s = [held([P, S], U8, f"h_s{b}") for b in range(HP)]
+        cap = [held([P, S], F32, f"cap{t}") for t in range(MT)]
+        capped = [held([P, S], F32, f"capped{t}") for t in range(MT)]
 
-        def deal_scales(b):
+        def gather_tab_words(a):
+            nc.vector.tensor_copy(v_w[a][:], tab_w[a][:].bitcast(U32).indirect(list1[:]))
+
+        def gather_tab_scales(a):
+            nc.vector.tensor_copy(v_s[a][:], tab_s[:, a, :].indirect(list1[:]))
+
+        def gather_tab2_words(b, m0, m1):
+            nc.vector.tensor_copy(v2_w[b][:, m0:m1], tab2_w[b][:].bitcast(U32).indirect(list2[:, m0 // 16 : m1 // 16]))
+
+        def deal_nav_scales(b):
             nc.vector.tensor_copy(
-                w_sd[b][:].rearrange("p a (i m) -> p a i m", i=PACK),
-                w_s[:, :, PASS * b : PASS * (b + 1)].rearrange("p a (m i) -> p a i m", i=PACK),
+                nav_sd[b][:].rearrange("p a (i m) -> p a i m", i=PACK),
+                nav_s[:, :, PASS * b : PASS * (b + 1)].rearrange("p a (m i) -> p a i m", i=PACK),
+            )
+
+        def deal_leg_scales():
+            nc.vector.tensor_copy(
+                leg_sd[:].rearrange("p b (i m) -> p b i m", i=PACK),
+                leg_s[:].rearrange("p (b m i) -> p b i m", b=HP, i=PACK),
             )
 
         def deal_nav(b):
@@ -169,175 +178,116 @@ def tile_list_orienteering_leg_scores_kernel(
                 leg_w[b][:].bitcast(U32).rearrange("p a (m i) -> p a m i", i=PACK),
             )
 
-        def round_ter(a, b):
-            grouped = ring.tile([P, PACK * PASS], BF16, name="grouped", align_bytes=64, bufs=4)
-            dst = grouped[:].rearrange("p (i m j) -> p m j i", i=PACK, j=PACK)
-            src = ter_f[a, b][:].rearrange("p j (m i) -> p m j i", i=PACK)
-            cut = VECTOR_SHARE[a, b]
-            if cut > 0:
-                nc.vector.tensor_copy(dst[:, :cut], src[:, :cut])
-            if cut < P:
-                nc.scalar.copy(dst[:, cut:], src[:, cut:])
-            return grouped
+        def round_ter(copy, rounded, m0, raw):
+            src = raw.rearrange("p j (m i) -> p m j i", i=PACK)
+            copy(rounded[:].rearrange("p (i m j) -> p m j i", i=PACK, j=PACK)[:, m0 : m0 + src.shape[1]], src)
 
-        def quantise_ter(a, b, grouped):
-            nc.vector.quantize_mx(out=ter_q[a, b][:].bitcast(FP8X4), scales=ter_s[a, b][:], in_=grouped[:])
+        def quantise(words, scales, values):
+            nc.vector.quantize_mx(out=words[:].bitcast(FP8X4), scales=scales[:], in_=values[:])
 
-        def pair_product(name, bufs, words, scales, i0, u):
-            bank = psum.tile([P, 2, HALF], F32, name=name, bufs=bufs)
-            cols = slice(HALF * u, HALF * (u + 1))
-            for a in range(KP):
-                for d in range(2):
-                    i = i0 + d
-                    nc.tensor.matmul_mx(
-                        out=bank[:, d, :],
-                        lhsT=words(a, i),
-                        lhsT_scale=scales(a, i),
-                        rhs=v_w[a][:, cols].bitcast(FP8X4),
-                        rhs_scale=v_s[a][:, cols],
-                        start=(a == 0 and d == 0),
-                        stop=(a == KP - 1 and d == 1),
-                    )
+        def product(words, scales, moving_words, moving_scales):
+            bank = psum.tile([P, S], F32, name="bank")
+            for g in range(2):
+                nc.tensor.matmul_mx(
+                    out=bank[:],
+                    lhsT=words(g),
+                    lhsT_scale=scales(g),
+                    rhs=moving_words[g][:].bitcast(FP8X4),
+                    rhs_scale=moving_scales[g][:],
+                    start=(g == 0),
+                    stop=(g == 1),
+                )
             return bank
 
-        def nav_stage(b, u):
-            for i0 in (0, 2):
-                bank = pair_product(
-                    "bank_a", 2,
-                    lambda a, i: nav_d[b][:, a, 2 * P * i : 2 * P * (i + 1)].bitcast(FP4X4),
-                    lambda a, i: w_sd[b][:, a, P * i : P * (i + 1)],
-                    i0, u,
+        def nav_products(b, nav_f):
+            for i in range(PACK):
+                bank = product(
+                    lambda a: nav_d[b][:, a, 2 * P * i : 2 * P * (i + 1)].bitcast(FP4X4),
+                    lambda a: nav_sd[b][:, a, P * i : P * (i + 1)],
+                    v_w, v_s,
                 )
-                nc.scalar.copy(nav_f[b, u][:, i0 : i0 + 2, :], bank[:])
+                nc.scalar.copy(nav_f[:, i, :], bank[:])
 
-        def join_max(b, u):
-            top = ring.tile([P, PACK, HALF], F32, name="top", bufs=4)
-            for i0 in (0, 2):
-                bank = pair_product(
-                    "bank_t", 3,
-                    lambda a, i: ter_q[a, b][:, P * i : P * (i + 1)].bitcast(FP8X4),
-                    lambda a, i: ter_s[a, b][:, P * i : P * (i + 1)],
-                    i0, u,
+        def join_max(b, nav_f):
+            for i in range(PACK):
+                bank = product(
+                    lambda a: ter_q[a, b][:, P * i : P * (i + 1)].bitcast(FP8X4),
+                    lambda a: ter_s[a, b][:, P * i : P * (i + 1)],
+                    v_w, v_s,
                 )
-                nc.vector.tensor_tensor(top[:, i0 : i0 + 2, :], bank[:], nav_f[b, u][:, i0 : i0 + 2, :], ALU.max)
-            return top
+                nc.vector.tensor_tensor(top[i][:], bank[:], nav_f[:, i, :], ALU.max)
 
-        def join_leg(b, u, top):
-            planes = ring.tile([P, PACK, HALF], BF16, name="planes", bufs=4)
-            for i0 in (0, 2):
-                bank = pair_product(
-                    "bank_l", 3,
-                    lambda a, i: leg_d[b][:, a, P * i : P * (i + 1)].bitcast(FP8X4),
-                    lambda a, i: w_sd[b][LEG_ROW:, a, P * i : P * (i + 1)],
-                    i0, u,
+        def join_leg(b):
+            for i in range(PACK):
+                bank = product(
+                    lambda a: leg_d[b][:, a, P * i : P * (i + 1)].bitcast(FP8X4),
+                    lambda a: leg_sd[LEG_ROW + 4 * a :, b, P * i : P * (i + 1)],
+                    v_w, v_s,
                 )
-                for d in range(2):
-                    i = i0 + d
-                    nc.vector.scalar_tensor_tensor(
-                        planes[:, i, :], top[:, i, :], gain_t[:, b, i : i + 1], bank[:, d, :], ALU.mult, ALU.add
-                    )
-            return planes
+                nc.vector.scalar_tensor_tensor(
+                    planes[b][:, i, :], top[i][:], gain_t[:, b, i : i + 1], bank[:], ALU.mult, ALU.add
+                )
 
-        def weave(planes):
-            woven = ring.tile([P, PACK * HALF], BF16, name="woven", align_bytes=64, bufs=4)
+        def weave(b, woven):
             nc.scalar.copy(
                 woven[:].rearrange("p (c n i) -> p c i n", n=4, i=PACK),
-                planes[:].rearrange("p i (c n) -> p c i n", n=4),
+                planes[b][:].rearrange("p i (c n) -> p c i n", n=4),
             )
-            return woven
 
-        def quantise_h(b, u, woven):
-            nc.vector.quantize_mx(out=h_q[b, u][:].bitcast(FP8X4), scales=h_s[b, u][:], in_=woven[:])
+        def stage(name):
+            return keep.tile([P, PACK * PASS], BF16, name=name, align_bytes=64)
 
-        cap = [held([P, S], F32, f"cap{t}") for t in range(MT)]
-
-        def score(u):
-            cols = slice(HALF * u, HALF * (u + 1))
-            capped = []
-            for t0 in (0, 2):
-                bank = psum.tile([P, 2, HALF], F32, name="bank_a", bufs=2)
-                for b in range(HP):
-                    for d in range(2):
-                        t = t0 + d
-                        nc.tensor.matmul_mx(
-                            out=bank[:, d, :],
-                            lhsT=v2_w[b][:, P * t : P * (t + 1)].bitcast(FP8X4),
-                            lhsT_scale=v2_s[TAB2_ROW + 4 * b :, P * t : P * (t + 1)],
-                            rhs=h_q[b, u][:].bitcast(FP8X4),
-                            rhs_scale=h_s[b, u][:],
-                            start=(b == 0 and d == 0),
-                            stop=(b == HP - 1 and d == 1),
-                        )
-                for d in range(2):
-                    t = t0 + d
-                    y = ring.tile([P, HALF], F32, name="y", bufs=8)
-                    nc.vector.scalar_tensor_tensor(
-                        y[:], bank[:, d, :], arch_t[:, t : t + 1], cap[t][:, cols], ALU.add, ALU.min
-                    )
-                    capped.append(y)
-            return capped
-
-        def place(u, capped):
-            cols = slice(HALF * u, HALF * (u + 1))
-            entries = list3[:, HALF // 16 * u : HALF // 16 * (u + 1)]
-            for t in range(MT):
-                nc.vector.tensor_tensor(page[t][:].indirect(entries), capped[t][:], wgo_t[:, cols], ALU.mult)
-                if u == 1:
-                    nc.sync.dma_start(out[P * t : P * (t + 1), :], page[t][:])
-
-        def add_arch(t):
-            nc.scalar.activation(cap[t][:], lim[t][:], ACT.Identity, bias=arch_t[:, t : t + 1])
-
-        def gather_tab2(b):
-            nc.vector.tensor_copy(v2_w[b][:], tab2_w[b][:].bitcast(U32).indirect(list2[:]))
-
-        gather_words(0, 0, S)
+        gather_tab_words(0)
         deal_nav(0)
-        g00 = round_ter(0, 0)
-        gather_scales(0)
-        gather_scales(1)
-        g10 = round_ter(1, 0)
-        quantise_ter(0, 0, g00)
-        deal_scales(0)
-        quantise_ter(1, 0, g10)
-        gather_words(1, 0, HALF)
-        gather_words(1, HALF, S)
-        nav_stage(0, 0)
-        top00 = join_max(0, 0)
-        nav_stage(0, 1)
+        gather_tab_scales(0)
+        gather_tab_scales(1)
+        rounded = stage("stage_a")
+        round_ter(nc.scalar.copy, rounded, 0, raw00[:])
+        deal_nav_scales(0)
+        gather_tab_words(1)
+        quantise(ter_q[0, 0], ter_s[0, 0], rounded)
+        rounded = stage("stage_b")
+        round_ter(nc.scalar.copy, rounded, 0, raw10a[:])
+        round_ter(nc.scalar.copy, rounded, P // 2, raw10b[:])
+        quantise(ter_q[1, 0], ter_s[1, 0], rounded)
+        nav_f = held([P, PACK, S], F32, f"ter_raw10_{P // 2}")
+        nav_products(0, nav_f)
+        deal_leg_scales()
+        deal_nav_scales(1)
         deal_leg(0)
-        top01 = join_max(0, 1)
-        deal_scales(1)
         deal_nav(1)
-        p00 = join_leg(0, 0, top00)
-        p01 = join_leg(0, 1, top01)
-        nav_stage(1, 0)
-        g01 = round_ter(0, 1)
-        nav_stage(1, 1)
-        g11 = round_ter(1, 1)
+        join_max(0, nav_f)
+        join_leg(0)
+        rounded = stage("stage_a")
+        round_ter(nc.scalar.copy, rounded, 0, raw01[:])
+        nav_f = held([P, PACK, S], F32, "nav_f1")
+        nav_products(1, nav_f)
+        quantise(ter_q[0, 1], ter_s[0, 1], rounded)
+        rounded = stage("stage_b")
+        round_ter(nc.vector.tensor_copy, rounded, 0, raw11[:])
+        quantise(ter_q[1, 1], ter_s[1, 1], rounded)
         deal_leg(1)
-        quantise_ter(0, 1, g01)
-        quantise_ter(1, 1, g11)
-        top10 = join_max(1, 0)
-        p10 = join_leg(1, 0, top10)
-        w00 = weave(p00)
-        w10 = weave(p10)
+        join_max(1, nav_f)
+        join_leg(1)
+        woven0 = stage("stage_b")
+        weave(0, woven0)
+        woven1 = stage("stage_a")
+        weave(1, woven1)
+        for t in range(MT):
+            nc.scalar.activation(cap[t][:], lim[t][:], ACT.Identity, bias=arch_t[:, t : t + 1])
         nc.vector.tensor_copy(v2_s[:], tab2_s[:].indirect(list2[:]))
-        gather_tab2(0)
-        gather_tab2(1)
-        top11 = join_max(1, 1)
-        p11 = join_leg(1, 1, top11)
-        add_arch(0)
-        add_arch(1)
-        w01 = weave(p01)
-        w11 = weave(p11)
-        add_arch(2)
-        add_arch(3)
-        quantise_h(0, 0, w00)
-        quantise_h(1, 0, w10)
-        first = score(0)
-        quantise_h(0, 1, w01)
-        quantise_h(1, 1, w11)
-        second = score(1)
-        place(0, first)
-        place(1, second)
+        gather_tab2_words(0, 0, S2)
+        quantise(h_q[0], h_s[0], woven0)
+        gather_tab2_words(1, 0, S2 // 2)
+        quantise(h_q[1], h_s[1], woven1)
+        gather_tab2_words(1, S2 // 2, S2)
+        for t in range(MT):
+            bank = product(
+                lambda b: v2_w[b][:, P * t : P * (t + 1)].bitcast(FP8X4),
+                lambda b: v2_s[TAB2_ROW + 4 * b :, P * t : P * (t + 1)],
+                h_q, h_s,
+            )
+            nc.vector.scalar_tensor_tensor(capped[t][:], bank[:], arch_t[:, t : t + 1], cap[t][:], ALU.add, ALU.min)
+        for t in range(MT):
+            nc.vector.tensor_tensor(page[t][:].indirect(list3[:]), capped[t][:], wgo_t[:], ALU.mult)
+            nc.sync.dma_start(out[P * t : P * (t + 1), :], page[t][:])

from contextlib import ExitStack

import concourse.mybir as mybir

K, T, S, H, T3, S2, T2 = 1024, 2048, 512, 1024, 1024, 512, 1024
FLOPS = 2 * (3 * K * H * S + H * S2 * S)

F32 = mybir.dt.float32
BF16 = mybir.dt.bfloat16
I32 = mybir.dt.int32
U32 = mybir.dt.uint32
U16 = mybir.dt.uint16
U8 = mybir.dt.uint8
FP8X4 = mybir.dt.float8_e4m3fn_x4
FP4X4 = mybir.dt.float4_e2m1fn_x4
ALU = mybir.AluOpType
ACT = mybir.ActivationFunctionType

P = 128
PACK = 4
PASS = P * PACK
KP = K // PASS
HP = H // PASS
MT = S2 // P
QUADS = 4
LEG_ROW = 4
TAB2_ROW = 8


def tile_list_orienteering_leg_scores_kernel(
    tc, tab_words, tab_scales, offs, tab2_words, tab2_scales, offs2, offs3, wter,
    wnav_words, wnav_scales, wleg_words, wleg_scales, gain, limit, arch, wgo, page1, out,
):
    nc = tc.nc
    with ExitStack() as ctx:
        keep = ctx.enter_context(tc.tile_pool(name="keep", bufs=1))
        psum = ctx.enter_context(tc.psum_pool(name="psum", bufs=8))

        def held(shape, dtype, name):
            return keep.tile(shape, dtype, name=name, align_bytes=64)

        list1 = keep.tile([P, S // 16], U16, name="list1")
        list2 = keep.tile([P, S2 // 16], U16, name="list2")
        list3 = keep.tile([P, S // 16], U16, name="list3")

        tab_w = [held([P, T], I32, f"tab_w{a}") for a in range(KP)]
        tab_s = held([P, KP, T], U8, "tab_s")
        tab2_w = [held([P, T3], I32, f"tab2_w{b}") for b in range(HP)]
        tab2_s = held([P, T3], U8, "tab2_s")
        nav_s = held([P, KP, H], U8, "nav_s")
        leg_s = held([P, H], U8, "leg_s")
        nav_w = [held([P, KP, 2 * PASS], U8, f"nav_w{b}") for b in range(HP)]
        leg_w = [held([P, KP, PASS], I32, f"leg_w{b}") for b in range(HP)]
        gain_t = held([P, HP, PACK], F32, "gain_t")
        arch_t = held([P, MT], F32, "arch_t")
        wgo_t = held([P, S], F32, "wgo_t")
        lim = [held([P, S], F32, f"lim{t}") for t in range(MT)]
        page = [held([P, T2], F32, f"page{t}") for t in range(MT)]

        nc.gpsimd.memset(tab_s[:, 0, :].bitcast(I32), 0)
        nc.vector.memset(tab_s[:, 1, :].bitcast(I32), 0)
        nc.vector.memset(nav_s[:].bitcast(I32), 0)
        nc.vector.memset(leg_s[:].bitcast(I32), 0)
        nc.vector.memset(tab2_s[:].bitcast(I32), 0)

        def load_scales_side_by_side(dst, src):
            for r in range(4):
                nc.sync.dma_start(
                    dst[r:P:32].bitcast(I32),
                    src[:, r:16:4, :].rearrange("a q t -> q a t").bitcast(I32),
                )

        def load_scales_stacked(dst, row, src):
            for q in range(QUADS):
                nc.sync.dma_start(
                    dst[32 * q + row : 32 * q + row + 8].bitcast(I32),
                    src[:, 4 * q : 4 * q + 4, :].bitcast(I32),
                )

        def load_tab(a, c0, c1):
            nc.sync.dma_start(tab_w[a][:, c0:c1], tab_words[a, :, c0:c1, :].rearrange("p t i -> p (t i)").bitcast(I32))

        def load_nav(b):
            nc.sync.dma_start(
                nav_w[b][:].bitcast(I32),
                wnav_words[:, :, 2 * PASS * b : 2 * PASS * (b + 1)].rearrange("a p n -> p a n").bitcast(I32),
            )

        def load_leg(b):
            nc.sync.dma_start(
                leg_w[b][:],
                wleg_words[:, :, PASS * b : PASS * (b + 1), :].rearrange("a p c i -> p a (c i)").bitcast(I32),
            )

        def load_ter(a, b, m0, m1):
            raw = held([P, PACK, PACK * (m1 - m0)], F32, f"ter_raw{a}{b}_{m0}")
            cols = slice(PASS * b + PACK * m0, PASS * b + PACK * m1)
            nc.sync.dma_start(raw[:], wter[PASS * a : PASS * (a + 1), cols].rearrange("(p j) c -> p j c", j=PACK))
            return raw

        nc.sync.dma_start(list1[:], offs)
        nc.sync.dma_start(list2[:], offs2)
        nc.sync.dma_start(list3[:], offs3)
        for c in range(0, T, T // 4):
            load_tab(0, c, c + T // 4)
        load_nav(0)
        load_scales_side_by_side(tab_s, tab_scales)
        raw00 = load_ter(0, 0, 0, P)
        load_scales_side_by_side(nav_s, wnav_scales)
        load_tab(1, 0, T)
        raw10a = load_ter(1, 0, 0, P // 2)
        raw10b = load_ter(1, 0, P // 2, P)
        load_leg(0)
        load_scales_stacked(leg_s, LEG_ROW, wleg_scales)
        load_nav(1)
        nc.sync.dma_start(gain_t[:], gain.rearrange("(b p i) -> p b i", b=HP, i=PACK))
        raw01 = load_ter(0, 1, 0, P)
        raw11 = load_ter(1, 1, 0, P)
        load_leg(1)
        load_scales_stacked(tab2_s, TAB2_ROW, tab2_scales)
        with nc.allow_non_contiguous_dma(reason="one value of arch to a partition and row tile"):
            nc.sync.dma_start(arch_t[:], arch.rearrange("(t p) -> p t", p=P))
        nc.sync.dma_start(wgo_t[:], wgo)
        for t in range(MT):
            nc.sync.dma_start(lim[t][:], limit[P * t : P * (t + 1), :])
        for b in range(HP):
            nc.sync.dma_start(tab2_w[b][:], tab2_words[b].rearrange("p t i -> p (t i)").bitcast(I32))
        for t in range(MT):
            nc.sync.dma_start(page[t][:], page1[P * t : P * (t + 1), :])

        v_w = [held([P, S], U32, f"v_w{a}") for a in range(KP)]
        v_s = [held([P, S], U8, f"v_s{a}") for a in range(KP)]
        v2_w = [held([P, S2], U32, f"v2_w{b}") for b in range(HP)]
        v2_s = held([P, S2], U8, "v2_s")
        nav_d = [held([P, KP, 2 * PASS], U8, f"nav_d{b}") for b in range(HP)]
        leg_d = [held([P, KP, PASS], U32, f"leg_d{b}") for b in range(HP)]
        nav_sd = [held([P, KP, PASS], U8, f"nav_sd{b}") for b in range(HP)]
        leg_sd = held([P, HP, PASS], U8, "leg_sd")
        ter_q = {(a, b): held([P, PASS], U32, f"ter_q{a}{b}") for a in range(KP) for b in range(HP)}
        ter_s = {(a, b): held([P, PASS], U8, f"ter_s{a}{b}") for a in range(KP) for b in range(HP)}
        top = [held([P, S], F32, f"top{i}") for i in range(PACK)]
        planes = [held([P, PACK, S], BF16, f"planes{b}") for b in range(HP)]
        h_q = [held([P, S], U32, f"h_q{b}") for b in range(HP)]
        h_s = [held([P, S], U8, f"h_s{b}") for b in range(HP)]
        cap = [held([P, S], F32, f"cap{t}") for t in range(MT)]
        capped = [held([P, S], F32, f"capped{t}") for t in range(MT)]

        def gather_tab_words(a):
            nc.vector.tensor_copy(v_w[a][:], tab_w[a][:].bitcast(U32).indirect(list1[:]))

        def gather_tab_scales(a):
            nc.vector.tensor_copy(v_s[a][:], tab_s[:, a, :].indirect(list1[:]))

        def gather_tab2_words(b, m0, m1):
            nc.vector.tensor_copy(v2_w[b][:, m0:m1], tab2_w[b][:].bitcast(U32).indirect(list2[:, m0 // 16 : m1 // 16]))

        def deal_nav_scales(b):
            nc.vector.tensor_copy(
                nav_sd[b][:].rearrange("p a (i m) -> p a i m", i=PACK),
                nav_s[:, :, PASS * b : PASS * (b + 1)].rearrange("p a (m i) -> p a i m", i=PACK),
            )

        def deal_leg_scales():
            nc.vector.tensor_copy(
                leg_sd[:].rearrange("p b (i m) -> p b i m", i=PACK),
                leg_s[:].rearrange("p (b m i) -> p b i m", b=HP, i=PACK),
            )

        def deal_nav(b):
            nc.scalar.copy(
                nav_d[b][:].bitcast(U16).rearrange("p a (i m) -> p a i m", i=PACK),
                nav_w[b][:].bitcast(U16).rearrange("p a (m i) -> p a i m", i=PACK),
            )

        def deal_leg(b):
            nc.scalar.copy(
                leg_d[b][:].rearrange("p a (i m) -> p a m i", i=PACK),
                leg_w[b][:].bitcast(U32).rearrange("p a (m i) -> p a m i", i=PACK),
            )

        def round_ter(copy, rounded, m0, raw):
            src = raw.rearrange("p j (m i) -> p m j i", i=PACK)
            copy(rounded[:].rearrange("p (i m j) -> p m j i", i=PACK, j=PACK)[:, m0 : m0 + src.shape[1]], src)

        def quantise(words, scales, values):
            nc.vector.quantize_mx(out=words[:].bitcast(FP8X4), scales=scales[:], in_=values[:])

        def product(words, scales, moving_words, moving_scales):
            bank = psum.tile([P, S], F32, name="bank")
            for g in range(2):
                nc.tensor.matmul_mx(
                    out=bank[:],
                    lhsT=words(g),
                    lhsT_scale=scales(g),
                    rhs=moving_words[g][:].bitcast(FP8X4),
                    rhs_scale=moving_scales[g][:],
                    start=(g == 0),
                    stop=(g == 1),
                )
            return bank

        def nav_products(b, nav_f):
            for i in range(PACK):
                bank = product(
                    lambda a: nav_d[b][:, a, 2 * P * i : 2 * P * (i + 1)].bitcast(FP4X4),
                    lambda a: nav_sd[b][:, a, P * i : P * (i + 1)],
                    v_w, v_s,
                )
                nc.scalar.copy(nav_f[:, i, :], bank[:])

        def join_max(b, nav_f):
            for i in range(PACK):
                bank = product(
                    lambda a: ter_q[a, b][:, P * i : P * (i + 1)].bitcast(FP8X4),
                    lambda a: ter_s[a, b][:, P * i : P * (i + 1)],
                    v_w, v_s,
                )
                nc.vector.tensor_tensor(top[i][:], bank[:], nav_f[:, i, :], ALU.max)

        def join_leg(b):
            for i in range(PACK):
                bank = product(
                    lambda a: leg_d[b][:, a, P * i : P * (i + 1)].bitcast(FP8X4),
                    lambda a: leg_sd[LEG_ROW + 4 * a :, b, P * i : P * (i + 1)],
                    v_w, v_s,
                )
                nc.vector.scalar_tensor_tensor(
                    planes[b][:, i, :], top[i][:], gain_t[:, b, i : i + 1], bank[:], ALU.mult, ALU.add
                )

        def weave(b, woven):
            nc.scalar.copy(
                woven[:].rearrange("p (c n i) -> p c i n", n=4, i=PACK),
                planes[b][:].rearrange("p i (c n) -> p c i n", n=4),
            )

        def stage(name):
            return keep.tile([P, PACK * PASS], BF16, name=name, align_bytes=64)

        gather_tab_words(0)
        deal_nav(0)
        gather_tab_scales(0)
        gather_tab_scales(1)
        rounded = stage("stage_a")
        round_ter(nc.scalar.copy, rounded, 0, raw00[:])
        deal_nav_scales(0)
        gather_tab_words(1)
        quantise(ter_q[0, 0], ter_s[0, 0], rounded)
        rounded = stage("stage_b")
        round_ter(nc.scalar.copy, rounded, 0, raw10a[:])
        round_ter(nc.scalar.copy, rounded, P // 2, raw10b[:])
        quantise(ter_q[1, 0], ter_s[1, 0], rounded)
        nav_f = held([P, PACK, S], F32, f"ter_raw10_{P // 2}")
        nav_products(0, nav_f)
        deal_leg_scales()
        deal_nav_scales(1)
        deal_leg(0)
        deal_nav(1)
        join_max(0, nav_f)
        join_leg(0)
        rounded = stage("stage_a")
        round_ter(nc.scalar.copy, rounded, 0, raw01[:])
        nav_f = held([P, PACK, S], F32, "nav_f1")
        nav_products(1, nav_f)
        quantise(ter_q[0, 1], ter_s[0, 1], rounded)
        rounded = stage("stage_b")
        round_ter(nc.vector.tensor_copy, rounded, 0, raw11[:])
        quantise(ter_q[1, 1], ter_s[1, 1], rounded)
        deal_leg(1)
        join_max(1, nav_f)
        join_leg(1)
        woven0 = stage("stage_b")
        weave(0, woven0)
        woven1 = stage("stage_a")
        weave(1, woven1)
        for t in range(MT):
            nc.scalar.activation(cap[t][:], lim[t][:], ACT.Identity, bias=arch_t[:, t : t + 1])
        nc.vector.tensor_copy(v2_s[:], tab2_s[:].indirect(list2[:]))
        gather_tab2_words(0, 0, S2)
        quantise(h_q[0], h_s[0], woven0)
        gather_tab2_words(1, 0, S2 // 2)
        quantise(h_q[1], h_s[1], woven1)
        gather_tab2_words(1, S2 // 2, S2)
        for t in range(MT):
            bank = product(
                lambda b: v2_w[b][:, P * t : P * (t + 1)].bitcast(FP8X4),
                lambda b: v2_s[TAB2_ROW + 4 * b :, P * t : P * (t + 1)],
                h_q, h_s,
            )
            nc.vector.scalar_tensor_tensor(capped[t][:], bank[:], arch_t[:, t : t + 1], cap[t][:], ALU.add, ALU.min)
        for t in range(MT):
            nc.vector.tensor_tensor(page[t][:].indirect(list3[:]), capped[t][:], wgo_t[:], ALU.mult)
            nc.sync.dma_start(out[P * t : P * (t + 1), :], page[t][:])
